import numpy as np
import ml_dtypes


def mxq(x, axis, fmt="e4m3"):
    dtype, down = {"e4m3": (ml_dtypes.float8_e4m3fn, 7), "e5m2": (ml_dtypes.float8_e5m2, 14)}[fmt]
    v = np.moveaxis(np.asarray(x, np.float32).astype(ml_dtypes.bfloat16).astype(np.float64), axis, -1)
    blocks = v.reshape(v.shape[:-1] + (-1, 32))
    amax = np.abs(blocks).max(-1, keepdims=True)
    byte = np.maximum(np.where(amax > 0, np.frexp(amax)[1] - 1 + 127, 0) - down, 1)
    scale = np.exp2(byte - 127.0)
    codes = (blocks / scale).astype(np.float32).astype(dtype).astype(np.float64)
    return np.moveaxis((codes * scale).reshape(v.shape), -1, axis)


WIDE = False


def mx_kscale(k):
    if not WIDE:
        return np.ones(k)
    levels = np.array([10, -10, 5, -5, 0])
    if k % 512:
        return np.exp2(np.random.permutation(np.resize(levels, k // 32))).repeat(32)
    a = np.empty((k // 512, 16))
    for p in range(k // 512):
        a[p, :8] = np.random.permutation(np.resize(levels, 8))
        for g in range(8):
            far = levels[np.abs(levels - a[p, g]) >= 10]
            a[p, g + 8] = far[np.random.randint(len(far))]
    return np.exp2(a.ravel()).repeat(32)


def f64(x):
    return np.asarray(x).astype(np.float64)


def striped(idx):
    return np.tile(idx.reshape(-1, 16).T, (8, 1)).astype(np.uint16)


def unstriped(offs):
    return offs[:16].T.reshape(-1).astype(np.int64)


def striped8(idx):
    return np.concatenate([x.reshape(-1, 16).T for x in idx]).astype(np.uint16)


def runs(offs, k):
    lists = np.stack([offs[16 * r : 16 * r + 16].T.reshape(-1) for r in range(8)]).astype(np.int64)
    return lists[np.arange(k) % 512 // 64]


def pack_weight(w):
    k, n = w.shape
    w = f64(np.asarray(w, np.float32).astype(ml_dtypes.bfloat16)).reshape(k // 32, 32, n)
    amax = np.abs(w).max(1)
    byte = np.clip(np.where(amax > 0, np.frexp(amax)[1] - 1 + 127 - 7, 1), 1, 254)
    scaled = (w * np.exp2(127.0 - byte)[:, None, :]).reshape(k, n).astype(np.float32)
    words = np.ascontiguousarray(scaled.reshape(k // 512, 128, 4, n).transpose(0, 1, 3, 2)).astype(ml_dtypes.float8_e4m3fn).view(np.uint8)
    return words, np.ascontiguousarray(byte.astype(np.uint8).reshape(k // 512, 16, n))


def unpack_weight(words, scales):
    g, p, n, _ = words.shape
    vals = np.ascontiguousarray(words).view(ml_dtypes.float8_e4m3fn).astype(np.float64) * np.repeat(np.exp2(scales.astype(np.float64) - 127.0), 8, axis=1)[..., None]
    return vals.transpose(0, 1, 3, 2).reshape(g * 512, n)


E2M1 = np.array([0.0, 0.5, 1.0, 1.5, 2.0, 3.0, 4.0, 6.0, -0.0, -0.5, -1.0, -1.5, -2.0, -3.0, -4.0, -6.0])


def pack_fp4(w):
    k, n = w.shape
    w = f64(np.asarray(w, np.float32).astype(ml_dtypes.bfloat16)).reshape(k // 32, 32, n)
    amax = np.abs(w).max(1)
    mant, ex = np.frexp(amax / 6.0)
    byte = np.clip(np.where(amax > 0, np.where(mant > 0.5, ex, ex - 1) + 127, 1), 1, 254)
    scaled = (w * np.exp2(127.0 - byte)[:, None, :]).reshape(k, n).astype(np.float32)
    c = np.ascontiguousarray(scaled.reshape(k // 512, 128, 4, n).transpose(0, 1, 3, 2)).astype(ml_dtypes.float4_e2m1fn).view(np.uint8) & 0xF
    words = (c[..., 0::2] | (c[..., 1::2] << 4)).reshape(k // 512, 128, 2 * n)
    return np.ascontiguousarray(words), np.ascontiguousarray(byte.astype(np.uint8).reshape(k // 512, 16, n))


def unpack_fp4(words, scales):
    g, _, n = scales.shape
    words = np.ascontiguousarray(words).reshape(g, 128, n, 2)
    nib = np.empty((g, 128, n, 4), np.uint8)
    nib[..., 0::2] = words & 0xF
    nib[..., 1::2] = words >> 4
    vals = E2M1[nib] * np.repeat(np.exp2(scales.astype(np.float64) - 127.0), 8, axis=1)[..., None]
    return vals.transpose(0, 1, 3, 2).reshape(g * 512, n)


def planes(y):
    n, m = y.shape
    v = y.astype(np.float32).astype(ml_dtypes.bfloat16).astype(np.float64).reshape(n // 32, 32, m)
    top = np.abs(v).max(1)
    byte = np.clip(np.where(top > 0, np.frexp(top)[1] - 1 + 127 - 7, 1), 1, 254)
    codes = (v * np.exp2(127.0 - byte)[:, None, :]).reshape(n, m).astype(np.float32).astype(ml_dtypes.float8_e4m3fn).view(np.uint8)
    words = codes.reshape(n // 512, 128, 4, m).transpose(0, 1, 3, 2)
    return np.ascontiguousarray(words), np.ascontiguousarray(byte.astype(np.uint8).reshape(n // 512, 16, m))


K, T, S, H = 512, 2048, 512, 512


def setup_inputs():
    n = np.random.standard_normal
    s = mx_kscale(K)[:, None]
    u = mx_kscale(S)
    packed_xT = pack_weight(n((K, T)) * s)
    packed_w1 = pack_fp4(n((K, H)) / np.sqrt(K) / s)
    return {
        "x_words": packed_xT[0],
        "x_scales": packed_xT[1],
        "w1_words": packed_w1[0],
        "w1_scales": packed_w1[1],
        "ga": (np.random.uniform(0.5, 1.5, (H, 1)) * u[:, None]).astype(np.float32),
        "gb": (np.random.uniform(0.5, 1.5, (H, 1)) / u[:, None]).astype(np.float32),
        "offs": striped(np.random.permutation(T)[:S]),
        "n1": striped8(np.stack([np.random.permutation(S) for _ in range(8)])),
        "n2": striped8(np.stack([np.random.permutation(S) for _ in range(8)])),
        "n3": striped8(np.stack([np.random.permutation(S) for _ in range(8)])),
        "n4": striped8(np.stack([np.random.permutation(S) for _ in range(8)])),
        "n5": striped8(np.stack([np.random.permutation(S) for _ in range(8)])),
        "n6": striped8(np.stack([np.random.permutation(S) for _ in range(8)])),
        "n7": striped8(np.stack([np.random.permutation(S) for _ in range(8)])),
    }


def reference(x_words, x_scales, w1_words, w1_scales, ga, gb, offs, n1, n2, n3, n4, n5, n6, n7):
    xq = unpack_weight(x_words, x_scales)[:, unstriped(offs)]
    y = unpack_fp4(w1_words, w1_scales).T @ xq
    sq = (y) ** 2
    z = f64(ga) * ((y[np.arange(H)[:, None], runs(n2, H)]) / (np.sqrt(sq + sq[np.arange(H)[:, None], runs(n1, H)] + 0.25)))
    pa = y[np.arange(H)[:, None], runs(n3, H)]
    kr = np.exp(-0.5 * ((y - pa) ** 2))
    pb = y[np.arange(H)[:, None], runs(n4, H)]
    kr2 = np.exp(-0.5 * ((y - pb) ** 2))
    z2 = f64(gb) * ((kr * pa + kr2 * pb) / (kr + kr2 + 0.5))
    s = 0.0625 * ((mxq(z, 0, "e4m3").T @ mxq(z2, 0, "e4m3")))
    st = s - (s[np.arange(S)[:, None], runs(n5, S)])
    su = np.maximum(st, st[np.arange(S)[:, None], runs(n6, S)])
    out_0 = su + 0.5 * (su[np.arange(S)[:, None], runs(n7, S)])
    return (out_0,) + planes(out_0)

@@ -1,0 +1,260 @@
+from contextlib import ExitStack
+
+import concourse.mybir as mybir
+from concourse.masks import make_identity
+
+F32 = mybir.dt.float32
+BF16 = mybir.dt.bfloat16
+I32 = mybir.dt.int32
+U32 = mybir.dt.uint32
+U16 = mybir.dt.uint16
+U8 = mybir.dt.uint8
+FP8X4 = mybir.dt.float8_e4m3fn_x4
+FP4X4 = mybir.dt.float4_e2m1fn_x4
+ALU = mybir.AluOpType
+ACT = mybir.ActivationFunctionType
+
+P = 128
+PACK = 4
+T = 2048
+S = 512
+WIN = 2 * S
+HALF = S // 2
+FLOPS = 2 * 2 * 512 * 512 * 512
+
+
+def tile_picked_selfrmskernthree_none_po_kernel(
+    tc, x_words, x_scales, w1_words, w1_scales, ga, gb, offs, n1, n2, n3, n4, n5, n6, n7, out_0, out_1, out_2
+):
+    nc = tc.nc
+    with ExitStack() as ctx:
+        keep = ctx.enter_context(tc.tile_pool(name="keep", bufs=1))
+        rows = ctx.enter_context(tc.tile_pool(name="rows", bufs=PACK))
+        ring = ctx.enter_context(tc.tile_pool(name="ring", bufs=3))
+        psum = ctx.enter_context(tc.psum_pool(name="psum", bufs=8))
+
+        def load_list(dram, name):
+            tile = keep.tile([P, S // 16], U16, name=name)
+            nc.sync.dma_start(tile[:], dram)
+            return tile
+
+        def load_scale_rows(queues, tile, dram):
+            for q, queue in enumerate(queues):
+                queue.dma_start(tile[32 * q : 32 * q + 4, :].bitcast(I32), dram[0, 4 * q : 4 * q + 4, :].bitcast(I32))
+
+        def turn(bank, sources):
+            for c in range(PACK):
+                cols = slice(c * P, (c + 1) * P)
+                for i, src in enumerate(sources):
+                    nc.tensor.matmul(
+                        bank[:, cols], lhsT=src[:, cols], rhs=ident[:], is_transpose=True,
+                        start=(i == 0), stop=(i == len(sources) - 1),
+                    )
+
+        def product(codes, scales, moving, moving_scales, pieces):
+            parts = []
+            for h in range(pieces):
+                cols = slice(h * S // pieces, (h + 1) * S // pieces)
+                bank = psum.tile([P, S // pieces], F32, tag="bank", name="product")
+                nc.tensor.matmul_mx(
+                    out=bank[:], lhsT=codes, lhsT_scale=scales, rhs=moving[:, cols].bitcast(FP8X4),
+                    rhs_scale=moving_scales[:, cols], start=True, stop=True,
+                )
+                parts.append((bank[:], cols))
+            return parts
+
+        xs = keep.tile([P, T], U8, align_bytes=64)
+        ws = keep.tile([P, S], U8, align_bytes=64)
+        nc.gpsimd.memset(xs[:].bitcast(I32), 0)
+        nc.gpsimd.memset(ws[:].bitcast(I32), 0)
+        warm = keep.tile([P, 1], F32)
+        nc.gpsimd.memset(warm[:], 0.0)
+
+        ww = keep.tile([P, 2 * S], U8, align_bytes=64)
+        nc.sync.dma_start(ww[:].bitcast(I32), w1_words[0].bitcast(I32))
+        l_offs = load_list(offs, "l_offs")
+        l3 = load_list(n3, "l3")
+        xw = keep.tile([P, T], I32, align_bytes=64)
+        nc.sync.dma_start(xw[:], x_words[0].rearrange("p n t -> p (n t)").bitcast(I32))
+        load_scale_rows([nc.scalar] * 4, xs, x_scales)
+        load_scale_rows([nc.gpsimd, nc.sync, nc.sync, nc.sync], ws, w1_scales)
+        nc.scalar.activation(out=warm[:], in_=warm[:], func=ACT.Exp)
+        l4 = load_list(n4, "l4")
+        l1 = load_list(n1, "l1")
+        l2 = load_list(n2, "l2")
+        ga_sb = keep.tile([P, PACK], F32)
+        gb_sb = keep.tile([P, PACK], F32)
+        nc.sync.dma_start(ga_sb[:], ga.rearrange("(p t) o -> p (t o)", t=PACK))
+        nc.sync.dma_start(gb_sb[:], gb.rearrange("(p t) o -> p (t o)", t=PACK))
+        l5 = load_list(n5, "l5")
+        l6 = load_list(n6, "l6")
+        l7 = load_list(n7, "l7")
+        ident = keep.tile([P, P], F32)
+        make_identity(nc, ident[:])
+
+        wwd = keep.tile([P, 2 * S], U8, align_bytes=64)
+        nc.vector.tensor_copy(
+            out=wwd[:].rearrange("p (t m b) -> p m t b", t=PACK, b=2),
+            in_=ww[:].rearrange("p (m t b) -> p m t b", t=PACK, b=2),
+        )
+        wsd = keep.tile([P, S], U8, align_bytes=64)
+        nc.vector.tensor_copy(
+            out=wsd[:].rearrange("p (t m) -> p m t", t=PACK), in_=ws[:].rearrange("p (m t) -> p m t", t=PACK)
+        )
+        xq = keep.tile([P, S], U32, align_bytes=64)
+        xqs = keep.tile([P, S], U8, align_bytes=64)
+        nc.vector.tensor_copy(out=xqs[:], in_=xs[:].indirect(l_offs[:]))
+        nc.vector.tensor_copy(out=xq[:], in_=xw[:].bitcast(U32).indirect(l_offs[:]))
+
+        y_win, y_twin = [], []
+        for t in range(PACK):
+            win = rows.tile([P, WIN], F32, tag="win_a", name="y_win")
+            twin = rows.tile([P, S], F32, tag="twin_a", name="y_twin")
+            parts = product(wwd[:, 2 * P * t : 2 * P * (t + 1)].bitcast(FP4X4), wsd[:, P * t : P * (t + 1)], xq, xqs, 2 if t == 0 else 1)
+            for bank, cols in parts:
+                nc.scalar.copy(out=win[:, cols], in_=bank)
+            if t == 0:
+                for bank, cols in reversed(parts):
+                    nc.vector.tensor_copy(out=twin[:, cols], in_=bank)
+            elif t == 1:
+                nc.scalar.copy(out=twin[:], in_=parts[0][0])
+            else:
+                nc.sync.dma_start(twin[:], win[:, :S])
+            y_win.append(win)
+            y_twin.append(twin)
+
+        sq_win, sq_twin, ga_win = [], [], []
+        weight, term = {}, {}
+        for t in range(PACK):
+            diff, flip = {}, {}
+            for side, lst in enumerate((l3, l4)):
+                diff[side] = rows.tile([P, S], F32, tag="diff%d" % side, name="diff")
+                nc.vector.tensor_tensor(out=diff[side][:], in0=y_win[t][:].indirect(lst[:]), in1=y_twin[t][:], op=ALU.subtract)
+            for side in range(2):
+                dsq = ring.tile([P, S], F32, name="dsq")
+                nc.scalar.activation(out=dsq[:], in_=diff[side][:], func=ACT.Square)
+                flip[side] = psum.tile([P, S], F32, tag="bank", name="flip")
+                turn(flip[side], [dsq])
+                if side == 0:
+                    win = rows.tile([P, WIN], F32, tag="win_b", name="sq_win")
+                    twin = rows.tile([P, S], F32, tag="twin_b", name="sq_twin")
+                    nc.scalar.activation(out=win[:, :S], in_=y_win[t][:, :S], func=ACT.Square)
+                    nc.sync.dma_start(twin[:], win[:, :S])
+                    sq_win.append(win)
+                    sq_twin.append(twin)
+            for side in range(2):
+                weight[t, side] = rows.tile([P, S], F32, tag="weight%d" % side, name="weight")
+                nc.scalar.activation(out=weight[t, side][:], in_=flip[side][:], func=ACT.Exp, scale=-0.5)
+                pick = flip[side]
+                turn(pick, [diff[side], y_twin[t]])
+                term[t, side] = rows.tile([P, S], F32, tag="term%d" % side, name="term")
+                nc.vector.tensor_tensor(out=term[t, side][:], in0=pick[:], in1=weight[t, side][:], op=ALU.mult)
+                if side == 0:
+                    win = rows.tile([P, WIN], F32, tag="win_c", name="ga_win")
+                    nc.scalar.activation(out=win[:, :S], in_=y_win[t][:, :S], func=ACT.Copy, scale=ga_sb[:, t : t + 1])
+                    ga_win.append(win)
+
+        quarter = keep.tile([P, 1], F32)
+        half = keep.tile([P, 1], F32)
+        last = weight[PACK - 1, 1][:, 0:1]
+        nc.scalar.activation(out=quarter[:], in_=last, func=ACT.Copy, scale=0.0, bias=0.25)
+        nc.scalar.activation(out=half[:], in_=last, func=ACT.Copy, scale=0.0, bias=0.5)
+
+        z = keep.tile([P, PACK, S], F32)
+        roots = []
+        for t in range(PACK):
+            root = rows.tile([P, S], F32, name="root")
+            nc.vector.tensor_tensor(out=root[:], in0=sq_win[t][:].indirect(l1[:]), in1=sq_twin[t][:], op=ALU.add)
+            nc.scalar.activation(out=root[:], in_=root[:], func=ACT.Abs_reciprocal_sqrt, bias=quarter[:])
+            roots.append(root)
+        for t in range(PACK):
+            nc.vector.tensor_tensor(out=z[:, t, :], in0=ga_win[t][:].indirect(l2[:]), in1=roots[t][:], op=ALU.mult)
+
+        z2 = keep.tile([P, PACK, S], F32)
+        recips = []
+        inv_root = keep.tile([P, PACK * S], F32, align_bytes=64)
+        for t in range(PACK):
+            den = psum.tile([P, S], F32, tag="bank", name="den")
+            turn(den, [weight[t, 0], weight[t, 1]])
+            recip = rows.tile([P, S], F32, name="recip")
+            nc.scalar.activation(out=inv_root[:, S * t : S * (t + 1)], in_=den[:], func=ACT.Abs_reciprocal_sqrt, bias=half[:])
+            nc.scalar.activation(out=recip[:], in_=inv_root[:, S * t : S * (t + 1)], func=ACT.Square)
+            recips.append(recip)
+        for t in range(PACK):
+            num = psum.tile([P, S], F32, tag="bank", name="num")
+            turn(num, [term[t, 0], term[t, 1]])
+            nc.vector.scalar_tensor_tensor(
+                out=z2[:, t, :], in0=num[:], scalar=gb_sb[:, t : t + 1], in1=recips[t][:], op0=ALU.mult, op1=ALU.mult
+            )
+        z_bf = inv_root[:, 2 * S :].bitcast(BF16)
+        nc.scalar.copy(
+            out=z_bf.rearrange("p (i m j) -> p m j i", i=PACK, j=PACK), in_=z[:].rearrange("p j (m i) -> p m j i", i=PACK)
+        )
+        z2_bf = keep.tile([P, PACK * S], BF16, align_bytes=64)
+        nc.vector.tensor_copy(
+            out=z2_bf[:].rearrange("p (m i j) -> p m j i", i=PACK, j=PACK), in_=z2[:].rearrange("p j (m i) -> p m j i", i=PACK)
+        )
+        z2q = keep.tile([P, S], U32, align_bytes=64)
+        z2qs = keep.tile([P, S], U8, align_bytes=64)
+        nc.vector.quantize_mx(out=z2q[:].bitcast(FP8X4), scales=z2qs[:], in_=z2_bf[:])
+
+        zq = keep.tile([P, S], U32, align_bytes=64)
+        zqs = keep.tile([P, S], U8, align_bytes=64)
+
+        neg_wins, s_rows = [], []
+        for t in range(PACK):
+            cols = slice(P * t, P * (t + 1))
+            nc.vector.quantize_mx(out=zq[:, cols].bitcast(FP8X4), scales=zqs[:, cols], in_=z_bf[:, S * t : S * (t + 1)])
+            parts = product(zq[:, cols].bitcast(FP8X4), zqs[:, cols], z2q, z2qs, 2 if t == 0 else 1)
+            neg_win = rows.tile([P, WIN], F32, tag="win_a", name="neg_win")
+            s = rows.tile([P, S], F32, tag="twin_a", name="s")
+            for bank, part in parts:
+                nc.scalar.activation(out=neg_win[:, part], in_=bank, func=ACT.Copy, scale=-0.0625)
+            for bank, part in reversed(parts):
+                if t == 0:
+                    nc.vector.tensor_scalar(out=s[:, part], in0=bank, scalar1=0.0625, scalar2=None, op0=ALU.mult)
+                else:
+                    nc.scalar.activation(out=s[:, part], in_=bank, func=ACT.Copy, scale=0.0625)
+            neg_wins.append(neg_win)
+            s_rows.append(s)
+        su, half_win = [], []
+        for pair in ((0, 1), (2, 3)):
+            st_win = {}
+            for t in pair:
+                st_win[t] = rows.tile([P, WIN], F32, tag="win_b", name="st_win")
+                nc.vector.tensor_tensor(out=st_win[t][:, :S], in0=neg_wins[t][:].indirect(l5[:]), in1=s_rows[t][:], op=ALU.add)
+            for t in pair:
+                nc.vector.tensor_copy(out=s_rows[t ^ 1][:], in_=st_win[t][:].indirect(l6[:]))
+            for t in pair:
+                top = rows.tile([P, S], F32, tag="twin_b", name="su")
+                nc.vector.tensor_tensor(out=top[:], in0=st_win[t][:, :S], in1=s_rows[t ^ 1][:], op=ALU.max)
+                win = rows.tile([P, WIN], F32, tag="win_c", name="half_win")
+                nc.scalar.activation(out=win[:, :S], in_=top[:], func=ACT.Copy, scale=0.5)
+                su.append(top)
+                half_win.append(win)
+
+        out_rows = out_0.rearrange("(p t) n -> p t n", t=PACK)
+        words = out_1[0].rearrange("p n t -> p (n t)").bitcast(I32)
+        oq = keep.tile([P, S], I32, align_bytes=64)
+        oqs = keep.tile([P, S], U8, align_bytes=64)
+        for h in range(2):
+            cols = slice(h * HALF, (h + 1) * HALF)
+            res = keep.tile([P, PACK, HALF], F32, name="res%d" % h)
+            for t in range(PACK):
+                nc.vector.tensor_tensor(
+                    out=res[:, t, :], in0=half_win[t][:].indirect(l7[:, h * HALF // 16 : (h + 1) * HALF // 16]),
+                    in1=su[t][:, cols], op=ALU.add,
+                )
+                nc.sync.dma_start(out_rows[:, t, cols], res[:, t, :])
+            res_bf = keep.tile([P, PACK * HALF], BF16, align_bytes=64, name="res_bf%d" % h)
+            dst = res_bf[:].rearrange("p (m i j) -> p m j i", i=PACK, j=PACK)
+            src = res[:].rearrange("p j (m i) -> p m j i", i=PACK)
+            if h == 0:
+                nc.scalar.copy(out=dst, in_=src)
+            else:
+                nc.vector.tensor_copy(out=dst, in_=src)
+            nc.vector.quantize_mx(out=oq[:, cols].bitcast(FP8X4), scales=oqs[:, cols], in_=res_bf[:])
+            nc.sync.dma_start(words[:, cols], oq[:, cols])
+        for q in range(4):
+            queue = nc.scalar if q % 2 else nc.sync
+            queue.dma_start(out_2[0, 4 * q : 4 * q + 4, :].bitcast(I32), oqs[32 * q : 32 * q + 4, :].bitcast(I32))

@@ -20,6 +20,8 @@ T = 2048
 S = 512
 WIN = 2 * S
 HALF = S // 2
+Z_SPLIT = 80
+CHUNKS = ((0, 256), (256, 384), (384, 512))
 FLOPS = 2 * 2 * 512 * 512 * 512
 
 
@@ -41,15 +43,6 @@ def tile_picked_selfrmskernthree_none_po_kernel(
         def load_scale_rows(queues, tile, dram):
             for q, queue in enumerate(queues):
                 queue.dma_start(tile[32 * q : 32 * q + 4, :].bitcast(I32), dram[0, 4 * q : 4 * q + 4, :].bitcast(I32))
-
-        def turn(bank, sources):
-            for c in range(PACK):
-                cols = slice(c * P, (c + 1) * P)
-                for i, src in enumerate(sources):
-                    nc.tensor.matmul(
-                        bank[:, cols], lhsT=src[:, cols], rhs=ident[:], is_transpose=True,
-                        start=(i == 0), stop=(i == len(sources) - 1),
-                    )
 
         def product(codes, scales, moving, moving_scales, pieces):
             parts = []
@@ -106,35 +99,30 @@ def tile_picked_selfrmskernthree_none_po_kernel(
         nc.vector.tensor_copy(out=xqs[:], in_=xs[:].indirect(l_offs[:]))
         nc.vector.tensor_copy(out=xq[:], in_=xw[:].bitcast(U32).indirect(l_offs[:]))
 
-        y_win, y_twin = [], []
+        y_win = []
         for t in range(PACK):
             win = rows.tile([P, WIN], F32, tag="win_a", name="y_win")
-            twin = rows.tile([P, S], F32, tag="twin_a", name="y_twin")
             parts = product(wwd[:, 2 * P * t : 2 * P * (t + 1)].bitcast(FP4X4), wsd[:, P * t : P * (t + 1)], xq, xqs, 2 if t == 0 else 1)
-            for bank, cols in parts:
-                nc.scalar.copy(out=win[:, cols], in_=bank)
-            if t == 0:
-                for bank, cols in reversed(parts):
-                    nc.vector.tensor_copy(out=twin[:, cols], in_=bank)
-            elif t == 1:
-                nc.scalar.copy(out=twin[:], in_=parts[0][0])
-            else:
-                nc.sync.dma_start(twin[:], win[:, :S])
+            for i, (bank, cols) in enumerate(parts):
+                if i == 0:
+                    nc.scalar.copy(out=win[:, cols], in_=bank)
+                else:
+                    nc.vector.tensor_copy(out=win[:, cols], in_=bank)
             y_win.append(win)
-            y_twin.append(twin)
 
         sq_win, sq_twin, ga_win = [], [], []
         weight, term = {}, {}
         for t in range(PACK):
-            diff, flip = {}, {}
+            pick, dsq = {}, {}
             for side, lst in enumerate((l3, l4)):
-                diff[side] = rows.tile([P, S], F32, tag="diff%d" % side, name="diff")
-                nc.vector.tensor_tensor(out=diff[side][:], in0=y_win[t][:].indirect(lst[:]), in1=y_twin[t][:], op=ALU.subtract)
+                pick[side] = rows.tile([P, S], F32, tag="pick%d" % side, name="pick")
+                nc.vector.tensor_copy(out=pick[side][:], in_=y_win[t][:].indirect(lst[:]))
             for side in range(2):
-                dsq = ring.tile([P, S], F32, name="dsq")
-                nc.scalar.activation(out=dsq[:], in_=diff[side][:], func=ACT.Square)
-                flip[side] = psum.tile([P, S], F32, tag="bank", name="flip")
-                turn(flip[side], [dsq])
+                diff = ring.tile([P, S], F32, name="diff")
+                engine = nc.vector if (t, side) == (PACK - 1, 1) else nc.gpsimd
+                engine.tensor_tensor(out=diff[:], in0=pick[side][:], in1=y_win[t][:, :S], op=ALU.subtract)
+                dsq[side] = ring.tile([P, S], F32, name="dsq")
+                nc.scalar.activation(out=dsq[side][:], in_=diff[:], func=ACT.Square)
                 if side == 0:
                     win = rows.tile([P, WIN], F32, tag="win_b", name="sq_win")
                     twin = rows.tile([P, S], F32, tag="twin_b", name="sq_twin")
@@ -144,11 +132,12 @@ def tile_picked_selfrmskernthree_none_po_kernel(
                     sq_twin.append(twin)
             for side in range(2):
                 weight[t, side] = rows.tile([P, S], F32, tag="weight%d" % side, name="weight")
-                nc.scalar.activation(out=weight[t, side][:], in_=flip[side][:], func=ACT.Exp, scale=-0.5)
-                pick = flip[side]
-                turn(pick, [diff[side], y_twin[t]])
+                nc.scalar.activation(out=weight[t, side][:], in_=dsq[side][:], func=ACT.Exp, scale=-0.5)
                 term[t, side] = rows.tile([P, S], F32, tag="term%d" % side, name="term")
-                nc.vector.tensor_tensor(out=term[t, side][:], in0=pick[:], in1=weight[t, side][:], op=ALU.mult)
+                nc.vector.scalar_tensor_tensor(
+                    out=term[t, side][:], in0=weight[t, side][:], scalar=gb_sb[:, t : t + 1], in1=pick[side][:],
+                    op0=ALU.mult, op1=ALU.mult,
+                )
                 if side == 0:
                     win = rows.tile([P, WIN], F32, tag="win_c", name="ga_win")
                     nc.scalar.activation(out=win[:, :S], in_=y_win[t][:, :S], func=ACT.Copy, scale=ga_sb[:, t : t + 1])
@@ -160,44 +149,58 @@ def tile_picked_selfrmskernthree_none_po_kernel(
         nc.scalar.activation(out=quarter[:], in_=last, func=ACT.Copy, scale=0.0, bias=0.25)
         nc.scalar.activation(out=half[:], in_=last, func=ACT.Copy, scale=0.0, bias=0.5)
 
-        z = keep.tile([P, PACK, S], F32)
+        def turned_sum(values, u, h, name):
+            bank = psum.tile([P, 2, 2, P], F32, tag="bank", name=name)
+            for c in range(2):
+                cols = slice((2 * h + c) * P, (2 * h + c + 1) * P)
+                for e in range(2):
+                    for side in range(2):
+                        nc.tensor.matmul(
+                            bank[:, c, e, :], lhsT=values[2 * u + e, side][:, cols], rhs=ident[:], is_transpose=True,
+                            start=(side == 0), stop=(side == 1),
+                        )
+            return bank[:].rearrange("n c e p -> n c p e")
+
         roots = []
         for t in range(PACK):
             root = rows.tile([P, S], F32, name="root")
             nc.vector.tensor_tensor(out=root[:], in0=sq_win[t][:].indirect(l1[:]), in1=sq_twin[t][:], op=ALU.add)
-            nc.scalar.activation(out=root[:], in_=root[:], func=ACT.Abs_reciprocal_sqrt, bias=quarter[:])
             roots.append(root)
-        for t in range(PACK):
-            nc.vector.tensor_tensor(out=z[:, t, :], in0=ga_win[t][:].indirect(l2[:]), in1=roots[t][:], op=ALU.mult)
 
-        z2 = keep.tile([P, PACK, S], F32)
-        recips = []
-        inv_root = keep.tile([P, PACK * S], F32, align_bytes=64)
+        z = keep.tile([P, PACK, S], F32)
+        z2_turned = {}
         for t in range(PACK):
-            den = psum.tile([P, S], F32, tag="bank", name="den")
-            turn(den, [weight[t, 0], weight[t, 1]])
-            recip = rows.tile([P, S], F32, name="recip")
-            nc.scalar.activation(out=inv_root[:, S * t : S * (t + 1)], in_=den[:], func=ACT.Abs_reciprocal_sqrt, bias=half[:])
-            nc.scalar.activation(out=recip[:], in_=inv_root[:, S * t : S * (t + 1)], func=ACT.Square)
-            recips.append(recip)
-        for t in range(PACK):
-            num = psum.tile([P, S], F32, tag="bank", name="num")
-            turn(num, [term[t, 0], term[t, 1]])
-            nc.vector.scalar_tensor_tensor(
-                out=z2[:, t, :], in0=num[:], scalar=gb_sb[:, t : t + 1], in1=recips[t][:], op0=ALU.mult, op1=ALU.mult
+            u, h = divmod(t, 2)
+            den = turned_sum(weight, u, h, "den")
+            num = turned_sum(term, u, h, "num")
+            inv_root = ring.tile([P, 2, P, 2], F32, name="inv_root")
+            recip = ring.tile([P, 2, P, 2], F32, name="recip")
+            nc.scalar.activation(out=inv_root[:], in_=den, func=ACT.Abs_reciprocal_sqrt, bias=half[:])
+            nc.scalar.activation(out=recip[:], in_=inv_root[:], func=ACT.Square)
+            z2_turned[u, h] = rows.tile([P, S], BF16, name="z2_turned")
+            nc.vector.tensor_tensor(
+                out=z2_turned[u, h][:].rearrange("n (c p e) -> n c p e", c=2, e=2), in0=num, in1=recip[:], op=ALU.mult
             )
-        z_bf = inv_root[:, 2 * S :].bitcast(BF16)
-        nc.scalar.copy(
-            out=z_bf.rearrange("p (i m j) -> p m j i", i=PACK, j=PACK), in_=z[:].rearrange("p j (m i) -> p m j i", i=PACK)
-        )
-        z2_bf = keep.tile([P, PACK * S], BF16, align_bytes=64)
-        nc.vector.tensor_copy(
-            out=z2_bf[:].rearrange("p (m i j) -> p m j i", i=PACK, j=PACK), in_=z2[:].rearrange("p j (m i) -> p m j i", i=PACK)
-        )
+            nc.scalar.activation(out=roots[t][:], in_=roots[t][:], func=ACT.Abs_reciprocal_sqrt, bias=quarter[:])
+            nc.vector.tensor_tensor(out=z[:, t, :], in0=ga_win[t][:].indirect(l2[:]), in1=roots[t][:], op=ALU.mult)
         z2q = keep.tile([P, S], U32, align_bytes=64)
         z2qs = keep.tile([P, S], U8, align_bytes=64)
-        nc.vector.quantize_mx(out=z2q[:].bitcast(FP8X4), scales=z2qs[:], in_=z2_bf[:])
-
+        for h in range(2):
+            bank = psum.tile([P, 2, HALF], F32, tag="bank", name="pairs")
+            for u in range(2):
+                for c in range(2):
+                    nc.tensor.transpose(
+                        bank[:, u, c * P : (c + 1) * P], z2_turned[u, h][:].bitcast(F32)[:, c * P : (c + 1) * P], ident[:]
+                    )
+            z2_bf = keep.tile([P, 2 * S], BF16, align_bytes=64, name="z2_bf%d" % h)
+            nc.scalar.copy(out=z2_bf[:].bitcast(F32).rearrange("p (n u) -> p n u", u=2), in_=bank[:].rearrange("p u n -> p n u"))
+            cols = slice(h * HALF, (h + 1) * HALF)
+            nc.vector.quantize_mx(out=z2q[:, cols].bitcast(FP8X4), scales=z2qs[:, cols], in_=z2_bf[:])
+        z_bf = keep.tile([P, PACK * S], BF16, align_bytes=64)
+        dealt = z_bf[:].rearrange("p (i m j) -> p m j i", i=PACK, j=PACK)
+        plain = z[:].rearrange("p j (m i) -> p m j i", i=PACK)
+        nc.vector.tensor_copy(out=dealt[:, :Z_SPLIT], in_=plain[:, :Z_SPLIT])
+        nc.scalar.copy(out=dealt[:, Z_SPLIT:], in_=plain[:, Z_SPLIT:])
         zq = keep.tile([P, S], U32, align_bytes=64)
         zqs = keep.tile([P, S], U8, align_bytes=64)
 
@@ -228,8 +231,8 @@ def tile_picked_selfrmskernthree_none_po_kernel(
             for t in pair:
                 top = rows.tile([P, S], F32, tag="twin_b", name="su")
                 nc.vector.tensor_tensor(out=top[:], in0=st_win[t][:, :S], in1=s_rows[t ^ 1][:], op=ALU.max)
-                win = rows.tile([P, WIN], F32, tag="win_c", name="half_win")
-                nc.scalar.activation(out=win[:, :S], in_=top[:], func=ACT.Copy, scale=0.5)
+                win = rows.tile([P, S], F32, tag="win_c", name="half_win")
+                nc.scalar.activation(out=win[:], in_=top[:], func=ACT.Copy, scale=0.5)
                 su.append(top)
                 half_win.append(win)
 
@@ -237,24 +240,22 @@ def tile_picked_selfrmskernthree_none_po_kernel(
         words = out_1[0].rearrange("p n t -> p (n t)").bitcast(I32)
         oq = keep.tile([P, S], I32, align_bytes=64)
         oqs = keep.tile([P, S], U8, align_bytes=64)
-        for h in range(2):
-            cols = slice(h * HALF, (h + 1) * HALF)
-            res = keep.tile([P, PACK, HALF], F32, name="res%d" % h)
+        for lo, hi in CHUNKS:
+            res = keep.tile([P, PACK, hi - lo], F32, name="res%d" % lo)
             for t in range(PACK):
                 nc.vector.tensor_tensor(
-                    out=res[:, t, :], in0=half_win[t][:].indirect(l7[:, h * HALF // 16 : (h + 1) * HALF // 16]),
-                    in1=su[t][:, cols], op=ALU.add,
+                    out=res[:, t, :], in0=half_win[t][:].indirect(l7[:, lo // 16 : hi // 16]), in1=su[t][:, lo:hi], op=ALU.add
                 )
-                nc.sync.dma_start(out_rows[:, t, cols], res[:, t, :])
-            res_bf = keep.tile([P, PACK * HALF], BF16, align_bytes=64, name="res_bf%d" % h)
+            nc.sync.dma_start(out_rows[:, :, lo:hi], res[:])
+            res_bf = keep.tile([P, PACK * (hi - lo)], BF16, align_bytes=64, name="res_bf%d" % lo)
             dst = res_bf[:].rearrange("p (m i j) -> p m j i", i=PACK, j=PACK)
             src = res[:].rearrange("p j (m i) -> p m j i", i=PACK)
-            if h == 0:
+            if hi < S:
                 nc.scalar.copy(out=dst, in_=src)
             else:
                 nc.vector.tensor_copy(out=dst, in_=src)
-            nc.vector.quantize_mx(out=oq[:, cols].bitcast(FP8X4), scales=oqs[:, cols], in_=res_bf[:])
-            nc.sync.dma_start(words[:, cols], oq[:, cols])
+            nc.vector.quantize_mx(out=oq[:, lo:hi].bitcast(FP8X4), scales=oqs[:, lo:hi], in_=res_bf[:])
+            nc.sync.dma_start(words[:, lo:hi], oq[:, lo:hi])
         for q in range(4):
             queue = nc.scalar if q % 2 else nc.sync
             queue.dma_start(out_2[0, 4 * q : 4 * q + 4, :].bitcast(I32), oqs[32 * q : 32 * q + 4, :].bitcast(I32))

@@ -21,6 +21,7 @@ S = 512
 WIN = 2 * S
 HALF = S // 2
 Z_SPLIT = 80
+TURNED = 3
 CHUNKS = ((0, 256), (256, 384), (384, 512))
 FLOPS = 2 * 2 * 512 * 512 * 512
 
@@ -44,6 +45,15 @@ def tile_picked_selfrmskernthree_none_po_kernel(
             for q, queue in enumerate(queues):
                 queue.dma_start(tile[32 * q : 32 * q + 4, :].bitcast(I32), dram[0, 4 * q : 4 * q + 4, :].bitcast(I32))
 
+        def turn(bank, sources):
+            for c in range(PACK):
+                cols = slice(c * P, (c + 1) * P)
+                for i, src in enumerate(sources):
+                    nc.tensor.matmul(
+                        bank[:, cols], lhsT=src[:, cols], rhs=ident[:], is_transpose=True,
+                        start=(i == 0), stop=(i == len(sources) - 1),
+                    )
+
         def product(codes, scales, moving, moving_scales, pieces):
             parts = []
             for h in range(pieces):
@@ -66,12 +76,14 @@ def tile_picked_selfrmskernthree_none_po_kernel(
         ww = keep.tile([P, 2 * S], U8, align_bytes=64)
         nc.sync.dma_start(ww[:].bitcast(I32), w1_words[0].bitcast(I32))
         l_offs = load_list(offs, "l_offs")
-        l3 = load_list(n3, "l3")
         xw = keep.tile([P, T], I32, align_bytes=64)
-        nc.sync.dma_start(xw[:], x_words[0].rearrange("p n t -> p (n t)").bitcast(I32))
-        load_scale_rows([nc.scalar] * 4, xs, x_scales)
-        load_scale_rows([nc.gpsimd, nc.sync, nc.sync, nc.sync], ws, w1_scales)
+        x_rows = x_words[0].rearrange("p n t -> p (n t)").bitcast(I32)
+        nc.sync.dma_start(xw[:, : T // 2], x_rows[:, : T // 2])
+        load_scale_rows([nc.sync] * 4, xs, x_scales)
+        nc.sync.dma_start(xw[:, T // 2 :], x_rows[:, T // 2 :])
+        load_scale_rows([nc.sync] * 4, ws, w1_scales)
         nc.scalar.activation(out=warm[:], in_=warm[:], func=ACT.Exp)
+        l3 = load_list(n3, "l3")
         l4 = load_list(n4, "l4")
         l1 = load_list(n1, "l1")
         l2 = load_list(n2, "l2")
@@ -91,15 +103,20 @@ def tile_picked_selfrmskernthree_none_po_kernel(
             in_=ww[:].rearrange("p (m t b) -> p m t b", t=PACK, b=2),
         )
         wsd = keep.tile([P, S], U8, align_bytes=64)
-        nc.vector.tensor_copy(
-            out=wsd[:].rearrange("p (t m) -> p m t", t=PACK), in_=ws[:].rearrange("p (m t) -> p m t", t=PACK)
-        )
+        dealt_scales = wsd[:].rearrange("p (t m) -> p m t", t=PACK)
+        plain_scales = ws[:].rearrange("p (m t) -> p m t", t=PACK)
+        nc.vector.tensor_copy(out=dealt_scales[:, :, :1], in_=plain_scales[:, :, :1])
+        nc.vector.tensor_copy(out=dealt_scales[:, :, 1:], in_=plain_scales[:, :, 1:])
         xq = keep.tile([P, S], U32, align_bytes=64)
         xqs = keep.tile([P, S], U8, align_bytes=64)
         nc.vector.tensor_copy(out=xqs[:], in_=xs[:].indirect(l_offs[:]))
-        nc.vector.tensor_copy(out=xq[:], in_=xw[:].bitcast(U32).indirect(l_offs[:]))
+        for h in range(2):
+            nc.vector.tensor_copy(
+                out=xq[:, h * HALF : (h + 1) * HALF],
+                in_=xw[:].bitcast(U32).indirect(l_offs[:, h * HALF // 16 : (h + 1) * HALF // 16]),
+            )
 
-        y_win = []
+        y_win, y_neg = [], []
         for t in range(PACK):
             win = rows.tile([P, WIN], F32, tag="win_a", name="y_win")
             parts = product(wwd[:, 2 * P * t : 2 * P * (t + 1)].bitcast(FP4X4), wsd[:, P * t : P * (t + 1)], xq, xqs, 2 if t == 0 else 1)
@@ -109,39 +126,72 @@ def tile_picked_selfrmskernthree_none_po_kernel(
                 else:
                     nc.vector.tensor_copy(out=win[:, cols], in_=bank)
             y_win.append(win)
+            if t < TURNED:
+                neg = rows.tile([P, S], F32, tag="twin_a", name="y_neg")
+                nc.scalar.activation(out=neg[:], in_=win[:, :S], func=ACT.Copy, scale=-1.0)
+                y_neg.append(neg)
 
-        sq_win, sq_twin, ga_win = [], [], []
-        weight, term = {}, {}
+        pick, diff = {}, {}
         for t in range(PACK):
-            pick, dsq = {}, {}
             for side, lst in enumerate((l3, l4)):
-                pick[side] = rows.tile([P, S], F32, tag="pick%d" % side, name="pick")
-                nc.vector.tensor_copy(out=pick[side][:], in_=y_win[t][:].indirect(lst[:]))
+                pick[t, side] = rows.tile([P, S], F32, tag="pick%d" % side, name="pick")
+                nc.vector.tensor_copy(out=pick[t, side][:], in_=y_win[t][:].indirect(lst[:]))
             for side in range(2):
-                diff = ring.tile([P, S], F32, name="diff")
-                engine = nc.vector if (t, side) == (PACK - 1, 1) else nc.gpsimd
-                engine.tensor_tensor(out=diff[:], in0=pick[side][:], in1=y_win[t][:, :S], op=ALU.subtract)
-                dsq[side] = ring.tile([P, S], F32, name="dsq")
-                nc.scalar.activation(out=dsq[side][:], in_=diff[:], func=ACT.Square)
-                if side == 0:
-                    win = rows.tile([P, WIN], F32, tag="win_b", name="sq_win")
-                    twin = rows.tile([P, S], F32, tag="twin_b", name="sq_twin")
-                    nc.scalar.activation(out=win[:, :S], in_=y_win[t][:, :S], func=ACT.Square)
-                    nc.sync.dma_start(twin[:], win[:, :S])
-                    sq_win.append(win)
-                    sq_twin.append(twin)
+                if t < TURNED:
+                    diff[t, side] = psum.tile([P, S], F32, tag="bank", name="diff_bank")
+                    turn(diff[t, side], [pick[t, side], y_neg[t]])
+                else:
+                    diff[t, side] = rows.tile([P, S], F32, name="diff")
+                    nc.vector.tensor_tensor(out=diff[t, side][:], in0=pick[t, side][:], in1=y_win[t][:, :S], op=ALU.subtract)
+        sq_win, sq_twin, ga_win = [], [], []
+        for t in range(PACK):
+            win = rows.tile([P, WIN], F32, tag="win_b", name="sq_win")
+            twin = rows.tile([P, S], F32, tag="twin_b", name="sq_twin")
+            nc.scalar.activation(out=win[:, :S], in_=y_win[t][:, :S], func=ACT.Square)
+            nc.sync.dma_start(twin[:], win[:, :S])
+            sq_win.append(win)
+            sq_twin.append(twin)
+        for t in range(PACK):
+            win = rows.tile([P, WIN], F32, tag="win_c", name="ga_win")
+            if t < PACK - 1:
+                nc.scalar.activation(out=win[:, :S], in_=y_win[t][:, :S], func=ACT.Copy, scale=ga_sb[:, t : t + 1])
+            else:
+                nc.vector.tensor_scalar(out=win[:, :S], in0=y_win[t][:, :S], scalar1=ga_sb[:, t : t + 1], scalar2=None, op0=ALU.mult)
+            ga_win.append(win)
+
+        dsq, weight, term, roots = {}, {}, {}, []
+
+        def square(t):
+            for side in range(2):
+                squared = rows.tile([P, S], F32, name="squared", bufs=5)
+                nc.scalar.activation(out=squared[:], in_=diff[t, side][:], func=ACT.Square)
+                if t < TURNED:
+                    turn(diff[t, side], [squared])
+                    dsq[t, side] = diff[t, side]
+                else:
+                    dsq[t, side] = squared
+
+        def weigh(t):
+            root = rows.tile([P, S], F32, tag="pick1" if t else "root", name="root")
+            nc.vector.tensor_tensor(out=root[:], in0=sq_win[t][:].indirect(l1[:]), in1=sq_twin[t][:], op=ALU.add)
+            roots.append(root)
             for side in range(2):
                 weight[t, side] = rows.tile([P, S], F32, tag="weight%d" % side, name="weight")
-                nc.scalar.activation(out=weight[t, side][:], in_=dsq[side][:], func=ACT.Exp, scale=-0.5)
+                nc.scalar.activation(out=weight[t, side][:], in_=dsq[t, side][:], func=ACT.Exp, scale=-0.5)
                 term[t, side] = rows.tile([P, S], F32, tag="term%d" % side, name="term")
                 nc.vector.scalar_tensor_tensor(
-                    out=term[t, side][:], in0=weight[t, side][:], scalar=gb_sb[:, t : t + 1], in1=pick[side][:],
+                    out=term[t, side][:], in0=weight[t, side][:], scalar=gb_sb[:, t : t + 1], in1=pick[t, side][:],
                     op0=ALU.mult, op1=ALU.mult,
                 )
-                if side == 0:
-                    win = rows.tile([P, WIN], F32, tag="win_c", name="ga_win")
-                    nc.scalar.activation(out=win[:, :S], in_=y_win[t][:, :S], func=ACT.Copy, scale=ga_sb[:, t : t + 1])
-                    ga_win.append(win)
+
+        square(0)
+        square(1)
+        square(2)
+        square(3)
+        weigh(0)
+        weigh(1)
+        weigh(2)
+        weigh(3)
 
         quarter = keep.tile([P, 1], F32)
         half = keep.tile([P, 1], F32)
@@ -161,25 +211,24 @@ def tile_picked_selfrmskernthree_none_po_kernel(
                         )
             return bank[:].rearrange("n c e p -> n c p e")
 
-        roots = []
-        for t in range(PACK):
-            root = rows.tile([P, S], F32, name="root")
-            nc.vector.tensor_tensor(out=root[:], in0=sq_win[t][:].indirect(l1[:]), in1=sq_twin[t][:], op=ALU.add)
-            roots.append(root)
+        den, num = {}, {}
+        for u in range(2):
+            for h in range(2):
+                den[u, h] = turned_sum(weight, u, h, "den")
+            for h in range(2):
+                num[u, h] = turned_sum(term, u, h, "num")
 
         z = keep.tile([P, PACK, S], F32)
         z2_turned = {}
         for t in range(PACK):
             u, h = divmod(t, 2)
-            den = turned_sum(weight, u, h, "den")
-            num = turned_sum(term, u, h, "num")
             inv_root = ring.tile([P, 2, P, 2], F32, name="inv_root")
             recip = ring.tile([P, 2, P, 2], F32, name="recip")
-            nc.scalar.activation(out=inv_root[:], in_=den, func=ACT.Abs_reciprocal_sqrt, bias=half[:])
+            nc.scalar.activation(out=inv_root[:], in_=den[u, h], func=ACT.Abs_reciprocal_sqrt, bias=half[:])
             nc.scalar.activation(out=recip[:], in_=inv_root[:], func=ACT.Square)
             z2_turned[u, h] = rows.tile([P, S], BF16, name="z2_turned")
             nc.vector.tensor_tensor(
-                out=z2_turned[u, h][:].rearrange("n (c p e) -> n c p e", c=2, e=2), in0=num, in1=recip[:], op=ALU.mult
+                out=z2_turned[u, h][:].rearrange("n (c p e) -> n c p e", c=2, e=2), in0=num[u, h], in1=recip[:], op=ALU.mult
             )
             nc.scalar.activation(out=roots[t][:], in_=roots[t][:], func=ACT.Abs_reciprocal_sqrt, bias=quarter[:])
             nc.vector.tensor_tensor(out=z[:, t, :], in0=ga_win[t][:].indirect(l2[:]), in1=roots[t][:], op=ALU.mult)
@@ -204,37 +253,69 @@ def tile_picked_selfrmskernthree_none_po_kernel(
         zq = keep.tile([P, S], U32, align_bytes=64)
         zqs = keep.tile([P, S], U8, align_bytes=64)
 
-        neg_wins, s_rows = [], []
+        banks, neg_win, s_rows, st_win, st_twin, rise, su_turned, su, half_win = {}, {}, {}, {}, {}, {}, {}, {}, {}
         for t in range(PACK):
             cols = slice(P * t, P * (t + 1))
             nc.vector.quantize_mx(out=zq[:, cols].bitcast(FP8X4), scales=zqs[:, cols], in_=z_bf[:, S * t : S * (t + 1)])
-            parts = product(zq[:, cols].bitcast(FP8X4), zqs[:, cols], z2q, z2qs, 2 if t == 0 else 1)
-            neg_win = rows.tile([P, WIN], F32, tag="win_a", name="neg_win")
-            s = rows.tile([P, S], F32, tag="twin_a", name="s")
-            for bank, part in parts:
-                nc.scalar.activation(out=neg_win[:, part], in_=bank, func=ACT.Copy, scale=-0.0625)
-            for bank, part in reversed(parts):
+            banks[t] = product(zq[:, cols].bitcast(FP8X4), zqs[:, cols], z2q, z2qs, 2 if t == 0 else 1)
+
+        def step(t):
+            neg_win[t] = rows.tile([P, WIN], F32, tag="win_a", name="neg_win")
+            s_rows[t] = rows.tile([P, S], F32, tag="twin_a", name="s")
+            for bank, part in banks[t]:
+                nc.scalar.activation(out=neg_win[t][:, part], in_=bank, func=ACT.Copy, scale=-0.0625)
+            for bank, part in reversed(banks[t]):
                 if t == 0:
-                    nc.vector.tensor_scalar(out=s[:, part], in0=bank, scalar1=0.0625, scalar2=None, op0=ALU.mult)
+                    nc.vector.tensor_scalar(out=s_rows[t][:, part], in0=bank, scalar1=0.0625, scalar2=None, op0=ALU.mult)
                 else:
-                    nc.scalar.activation(out=s[:, part], in_=bank, func=ACT.Copy, scale=0.0625)
-            neg_wins.append(neg_win)
-            s_rows.append(s)
-        su, half_win = [], []
-        for pair in ((0, 1), (2, 3)):
-            st_win = {}
-            for t in pair:
-                st_win[t] = rows.tile([P, WIN], F32, tag="win_b", name="st_win")
-                nc.vector.tensor_tensor(out=st_win[t][:, :S], in0=neg_wins[t][:].indirect(l5[:]), in1=s_rows[t][:], op=ALU.add)
-            for t in pair:
-                nc.vector.tensor_copy(out=s_rows[t ^ 1][:], in_=st_win[t][:].indirect(l6[:]))
-            for t in pair:
-                top = rows.tile([P, S], F32, tag="twin_b", name="su")
-                nc.vector.tensor_tensor(out=top[:], in0=st_win[t][:, :S], in1=s_rows[t ^ 1][:], op=ALU.max)
-                win = rows.tile([P, S], F32, tag="win_c", name="half_win")
-                nc.scalar.activation(out=win[:], in_=top[:], func=ACT.Copy, scale=0.5)
-                su.append(top)
-                half_win.append(win)
+                    nc.scalar.activation(out=s_rows[t][:, part], in_=bank, func=ACT.Copy, scale=0.0625)
+            st_win[t] = rows.tile([P, WIN], F32, tag="win_b", name="st_win")
+            nc.vector.tensor_tensor(out=st_win[t][:, :S], in0=neg_win[t][:].indirect(l5[:]), in1=s_rows[t][:], op=ALU.add)
+
+        def excess(t):
+            st_twin[t] = rows.tile([P, S], F32, tag="term0", name="st_twin")
+            nc.scalar.copy(out=st_twin[t][:], in_=st_win[t][:, :S])
+            rise[t] = rows.tile([P, S], F32, tag="term1", name="rise")
+            nc.vector.tensor_tensor(out=rise[t][:], in0=st_win[t][:].indirect(l6[:]), in1=st_twin[t][:], op=ALU.subtract)
+
+        def clip(t):
+            nc.scalar.activation(out=rise[t][:], in_=rise[t][:], func=ACT.Relu)
+            banks[t] = psum.tile([P, S], F32, tag="bank", name="su_bank")
+            turn(banks[t], [st_twin[t], rise[t]])
+
+        def turn_back(t):
+            su_turned[t] = rows.tile([P, S], F32, tag="weight0", name="su_turned")
+            nc.scalar.copy(out=su_turned[t][:], in_=banks[t][:])
+            turn(banks[t], [su_turned[t]])
+
+        def halve(t, source):
+            half_win[t] = rows.tile([P, S], F32, tag="win_c", name="half_win")
+            nc.scalar.activation(out=half_win[t][:], in_=source, func=ACT.Copy, scale=0.5)
+
+        def leave_bank(t):
+            su[t] = rows.tile([P, S], F32, tag="twin_b", name="su")
+            nc.scalar.copy(out=su[t][:], in_=banks[t][:])
+            halve(t, banks[t][:])
+
+        step(0)
+        step(1)
+        excess(0)
+        step(2)
+        excess(1)
+        clip(0)
+        step(3)
+        turn_back(0)
+        clip(1)
+        leave_bank(0)
+        turn_back(1)
+        for t in (2, 3):
+            nc.vector.tensor_copy(out=s_rows[t ^ 1][:], in_=st_win[t][:].indirect(l6[:]))
+        for t in (2, 3):
+            su[t] = rows.tile([P, S], F32, tag="twin_b", name="su")
+            nc.vector.tensor_tensor(out=su[t][:], in0=st_win[t][:, :S], in1=s_rows[t ^ 1][:], op=ALU.max)
+        halve(2, su[2][:])
+        leave_bank(1)
+        halve(3, su[3][:])
 
         out_rows = out_0.rearrange("(p t) n -> p t n", t=PACK)
         words = out_1[0].rearrange("p n t -> p (n t)").bitcast(I32)
@@ -242,7 +323,7 @@ def tile_picked_selfrmskernthree_none_po_kernel(
         oqs = keep.tile([P, S], U8, align_bytes=64)
         for lo, hi in CHUNKS:
             res = keep.tile([P, PACK, hi - lo], F32, name="res%d" % lo)
-            for t in range(PACK):
+            for t in (0, 2, 1, 3):
                 nc.vector.tensor_tensor(
                     out=res[:, t, :], in0=half_win[t][:].indirect(l7[:, lo // 16 : hi // 16]), in1=su[t][:, lo:hi], op=ALU.add
                 )

from contextlib import ExitStack

import concourse.mybir as mybir
from concourse.masks import make_identity

F32 = mybir.dt.float32
BF16 = mybir.dt.bfloat16
I32 = mybir.dt.int32
U32 = mybir.dt.uint32
U16 = mybir.dt.uint16
U8 = mybir.dt.uint8
FP8X4 = mybir.dt.float8_e4m3fn_x4
FP4X4 = mybir.dt.float4_e2m1fn_x4
ALU = mybir.AluOpType
ACT = mybir.ActivationFunctionType

P = 128
PACK = 4
T = 2048
S = 512
WIN = 2 * S
HALF = S // 2
Z_SPLIT = 80
TURNED = 3
CHUNKS = ((0, 256), (256, 384), (384, 512))
FLOPS = 2 * 2 * 512 * 512 * 512


def tile_picked_selfrmskernthree_none_po_kernel(
    tc, x_words, x_scales, w1_words, w1_scales, ga, gb, offs, n1, n2, n3, n4, n5, n6, n7, out_0, out_1, out_2
):
    nc = tc.nc
    with ExitStack() as ctx:
        keep = ctx.enter_context(tc.tile_pool(name="keep", bufs=1))
        rows = ctx.enter_context(tc.tile_pool(name="rows", bufs=PACK))
        ring = ctx.enter_context(tc.tile_pool(name="ring", bufs=3))
        psum = ctx.enter_context(tc.psum_pool(name="psum", bufs=8))

        def load_list(dram, name):
            tile = keep.tile([P, S // 16], U16, name=name)
            nc.sync.dma_start(tile[:], dram)
            return tile

        def load_scale_rows(queues, tile, dram):
            for q, queue in enumerate(queues):
                queue.dma_start(tile[32 * q : 32 * q + 4, :].bitcast(I32), dram[0, 4 * q : 4 * q + 4, :].bitcast(I32))

        def turn(bank, sources):
            for c in range(PACK):
                cols = slice(c * P, (c + 1) * P)
                for i, src in enumerate(sources):
                    nc.tensor.matmul(
                        bank[:, cols], lhsT=src[:, cols], rhs=ident[:], is_transpose=True,
                        start=(i == 0), stop=(i == len(sources) - 1),
                    )

        def product(codes, scales, moving, moving_scales, pieces):
            parts = []
            for h in range(pieces):
                cols = slice(h * S // pieces, (h + 1) * S // pieces)
                bank = psum.tile([P, S // pieces], F32, tag="bank", name="product")
                nc.tensor.matmul_mx(
                    out=bank[:], lhsT=codes, lhsT_scale=scales, rhs=moving[:, cols].bitcast(FP8X4),
                    rhs_scale=moving_scales[:, cols], start=True, stop=True,
                )
                parts.append((bank[:], cols))
            return parts

        xs = keep.tile([P, T], U8, align_bytes=64)
        ws = keep.tile([P, S], U8, align_bytes=64)
        nc.gpsimd.memset(xs[:].bitcast(I32), 0)
        nc.gpsimd.memset(ws[:].bitcast(I32), 0)
        warm = keep.tile([P, 1], F32)
        nc.gpsimd.memset(warm[:], 0.0)

        ww = keep.tile([P, 2 * S], U8, align_bytes=64)
        nc.sync.dma_start(ww[:].bitcast(I32), w1_words[0].bitcast(I32))
        l_offs = load_list(offs, "l_offs")
        xw = keep.tile([P, T], I32, align_bytes=64)
        x_rows = x_words[0].rearrange("p n t -> p (n t)").bitcast(I32)
        nc.sync.dma_start(xw[:, : T // 2], x_rows[:, : T // 2])
        load_scale_rows([nc.sync] * 4, xs, x_scales)
        nc.sync.dma_start(xw[:, T // 2 :], x_rows[:, T // 2 :])
        load_scale_rows([nc.sync] * 4, ws, w1_scales)
        nc.scalar.activation(out=warm[:], in_=warm[:], func=ACT.Exp)
        l3 = load_list(n3, "l3")
        l4 = load_list(n4, "l4")
        l1 = load_list(n1, "l1")
        l2 = load_list(n2, "l2")
        ga_sb = keep.tile([P, PACK], F32)
        gb_sb = keep.tile([P, PACK], F32)
        nc.sync.dma_start(ga_sb[:], ga.rearrange("(p t) o -> p (t o)", t=PACK))
        nc.sync.dma_start(gb_sb[:], gb.rearrange("(p t) o -> p (t o)", t=PACK))
        l5 = load_list(n5, "l5")
        l6 = load_list(n6, "l6")
        l7 = load_list(n7, "l7")
        ident = keep.tile([P, P], F32)
        make_identity(nc, ident[:])

        wwd = keep.tile([P, 2 * S], U8, align_bytes=64)
        nc.vector.tensor_copy(
            out=wwd[:].rearrange("p (t m b) -> p m t b", t=PACK, b=2),
            in_=ww[:].rearrange("p (m t b) -> p m t b", t=PACK, b=2),
        )
        wsd = keep.tile([P, S], U8, align_bytes=64)
        dealt_scales = wsd[:].rearrange("p (t m) -> p m t", t=PACK)
        plain_scales = ws[:].rearrange("p (m t) -> p m t", t=PACK)
        nc.vector.tensor_copy(out=dealt_scales[:, :, :1], in_=plain_scales[:, :, :1])
        nc.vector.tensor_copy(out=dealt_scales[:, :, 1:], in_=plain_scales[:, :, 1:])
        xq = keep.tile([P, S], U32, align_bytes=64)
        xqs = keep.tile([P, S], U8, align_bytes=64)
        nc.vector.tensor_copy(out=xqs[:], in_=xs[:].indirect(l_offs[:]))
        for h in range(2):
            nc.vector.tensor_copy(
                out=xq[:, h * HALF : (h + 1) * HALF],
                in_=xw[:].bitcast(U32).indirect(l_offs[:, h * HALF // 16 : (h + 1) * HALF // 16]),
            )

        y_win, y_neg = [], []
        for t in range(PACK):
            win = rows.tile([P, WIN], F32, tag="win_a", name="y_win")
            parts = product(wwd[:, 2 * P * t : 2 * P * (t + 1)].bitcast(FP4X4), wsd[:, P * t : P * (t + 1)], xq, xqs, 2 if t == 0 else 1)
            for i, (bank, cols) in enumerate(parts):
                if i == 0:
                    nc.scalar.copy(out=win[:, cols], in_=bank)
                else:
                    nc.vector.tensor_copy(out=win[:, cols], in_=bank)
            y_win.append(win)
            if t < TURNED:
                neg = rows.tile([P, S], F32, tag="twin_a", name="y_neg")
                nc.scalar.activation(out=neg[:], in_=win[:, :S], func=ACT.Copy, scale=-1.0)
                y_neg.append(neg)

        pick, diff = {}, {}
        for t in range(PACK):
            for side, lst in enumerate((l3, l4)):
                pick[t, side] = rows.tile([P, S], F32, tag="pick%d" % side, name="pick")
                nc.vector.tensor_copy(out=pick[t, side][:], in_=y_win[t][:].indirect(lst[:]))
            for side in range(2):
                if t < TURNED:
                    diff[t, side] = psum.tile([P, S], F32, tag="bank", name="diff_bank")
                    turn(diff[t, side], [pick[t, side], y_neg[t]])
                else:
                    diff[t, side] = rows.tile([P, S], F32, name="diff")
                    nc.vector.tensor_tensor(out=diff[t, side][:], in0=pick[t, side][:], in1=y_win[t][:, :S], op=ALU.subtract)
        sq_win, sq_twin, ga_win = [], [], []
        for t in range(PACK):
            win = rows.tile([P, WIN], F32, tag="win_b", name="sq_win")
            twin = rows.tile([P, S], F32, tag="twin_b", name="sq_twin")
            nc.scalar.activation(out=win[:, :S], in_=y_win[t][:, :S], func=ACT.Square)
            nc.sync.dma_start(twin[:], win[:, :S])
            sq_win.append(win)
            sq_twin.append(twin)
        for t in range(PACK):
            win = rows.tile([P, WIN], F32, tag="win_c", name="ga_win")
            if t < PACK - 1:
                nc.scalar.activation(out=win[:, :S], in_=y_win[t][:, :S], func=ACT.Copy, scale=ga_sb[:, t : t + 1])
            else:
                nc.vector.tensor_scalar(out=win[:, :S], in0=y_win[t][:, :S], scalar1=ga_sb[:, t : t + 1], scalar2=None, op0=ALU.mult)
            ga_win.append(win)

        dsq, weight, term, roots = {}, {}, {}, []

        def square(t):
            for side in range(2):
                squared = rows.tile([P, S], F32, name="squared", bufs=5)
                nc.scalar.activation(out=squared[:], in_=diff[t, side][:], func=ACT.Square)
                if t < TURNED:
                    turn(diff[t, side], [squared])
                    dsq[t, side] = diff[t, side]
                else:
                    dsq[t, side] = squared

        def weigh(t):
            root = rows.tile([P, S], F32, tag="pick1" if t else "root", name="root")
            nc.vector.tensor_tensor(out=root[:], in0=sq_win[t][:].indirect(l1[:]), in1=sq_twin[t][:], op=ALU.add)
            roots.append(root)
            for side in range(2):
                weight[t, side] = rows.tile([P, S], F32, tag="weight%d" % side, name="weight")
                nc.scalar.activation(out=weight[t, side][:], in_=dsq[t, side][:], func=ACT.Exp, scale=-0.5)
                term[t, side] = rows.tile([P, S], F32, tag="term%d" % side, name="term")
                nc.vector.scalar_tensor_tensor(
                    out=term[t, side][:], in0=weight[t, side][:], scalar=gb_sb[:, t : t + 1], in1=pick[t, side][:],
                    op0=ALU.mult, op1=ALU.mult,
                )

        square(0)
        square(1)
        square(2)
        square(3)
        weigh(0)
        weigh(1)
        weigh(2)
        weigh(3)

        quarter = keep.tile([P, 1], F32)
        half = keep.tile([P, 1], F32)
        last = weight[PACK - 1, 1][:, 0:1]
        nc.scalar.activation(out=quarter[:], in_=last, func=ACT.Copy, scale=0.0, bias=0.25)
        nc.scalar.activation(out=half[:], in_=last, func=ACT.Copy, scale=0.0, bias=0.5)

        def turned_sum(values, u, h, name):
            bank = psum.tile([P, 2, 2, P], F32, tag="bank", name=name)
            for c in range(2):
                cols = slice((2 * h + c) * P, (2 * h + c + 1) * P)
                for e in range(2):
                    for side in range(2):
                        nc.tensor.matmul(
                            bank[:, c, e, :], lhsT=values[2 * u + e, side][:, cols], rhs=ident[:], is_transpose=True,
                            start=(side == 0), stop=(side == 1),
                        )
            return bank[:].rearrange("n c e p -> n c p e")

        den, num = {}, {}
        for u in range(2):
            for h in range(2):
                den[u, h] = turned_sum(weight, u, h, "den")
            for h in range(2):
                num[u, h] = turned_sum(term, u, h, "num")

        z = keep.tile([P, PACK, S], F32)
        z2_turned = {}
        for t in range(PACK):
            u, h = divmod(t, 2)
            inv_root = ring.tile([P, 2, P, 2], F32, name="inv_root")
            recip = ring.tile([P, 2, P, 2], F32, name="recip")
            nc.scalar.activation(out=inv_root[:], in_=den[u, h], func=ACT.Abs_reciprocal_sqrt, bias=half[:])
            nc.scalar.activation(out=recip[:], in_=inv_root[:], func=ACT.Square)
            z2_turned[u, h] = rows.tile([P, S], BF16, name="z2_turned")
            nc.vector.tensor_tensor(
                out=z2_turned[u, h][:].rearrange("n (c p e) -> n c p e", c=2, e=2), in0=num[u, h], in1=recip[:], op=ALU.mult
            )
            nc.scalar.activation(out=roots[t][:], in_=roots[t][:], func=ACT.Abs_reciprocal_sqrt, bias=quarter[:])
            nc.vector.tensor_tensor(out=z[:, t, :], in0=ga_win[t][:].indirect(l2[:]), in1=roots[t][:], op=ALU.mult)
        z2q = keep.tile([P, S], U32, align_bytes=64)
        z2qs = keep.tile([P, S], U8, align_bytes=64)
        for h in range(2):
            bank = psum.tile([P, 2, HALF], F32, tag="bank", name="pairs")
            for u in range(2):
                for c in range(2):
                    nc.tensor.transpose(
                        bank[:, u, c * P : (c + 1) * P], z2_turned[u, h][:].bitcast(F32)[:, c * P : (c + 1) * P], ident[:]
                    )
            z2_bf = keep.tile([P, 2 * S], BF16, align_bytes=64, name="z2_bf%d" % h)
            nc.scalar.copy(out=z2_bf[:].bitcast(F32).rearrange("p (n u) -> p n u", u=2), in_=bank[:].rearrange("p u n -> p n u"))
            cols = slice(h * HALF, (h + 1) * HALF)
            nc.vector.quantize_mx(out=z2q[:, cols].bitcast(FP8X4), scales=z2qs[:, cols], in_=z2_bf[:])
        z_bf = keep.tile([P, PACK * S], BF16, align_bytes=64)
        dealt = z_bf[:].rearrange("p (i m j) -> p m j i", i=PACK, j=PACK)
        plain = z[:].rearrange("p j (m i) -> p m j i", i=PACK)
        nc.vector.tensor_copy(out=dealt[:, :Z_SPLIT], in_=plain[:, :Z_SPLIT])
        nc.scalar.copy(out=dealt[:, Z_SPLIT:], in_=plain[:, Z_SPLIT:])
        zq = keep.tile([P, S], U32, align_bytes=64)
        zqs = keep.tile([P, S], U8, align_bytes=64)

        banks, neg_win, s_rows, st_win, st_twin, rise, su_turned, su, half_win = {}, {}, {}, {}, {}, {}, {}, {}, {}
        for t in range(PACK):
            cols = slice(P * t, P * (t + 1))
            nc.vector.quantize_mx(out=zq[:, cols].bitcast(FP8X4), scales=zqs[:, cols], in_=z_bf[:, S * t : S * (t + 1)])
            banks[t] = product(zq[:, cols].bitcast(FP8X4), zqs[:, cols], z2q, z2qs, 2 if t == 0 else 1)

        def step(t):
            neg_win[t] = rows.tile([P, WIN], F32, tag="win_a", name="neg_win")
            s_rows[t] = rows.tile([P, S], F32, tag="twin_a", name="s")
            for bank, part in banks[t]:
                nc.scalar.activation(out=neg_win[t][:, part], in_=bank, func=ACT.Copy, scale=-0.0625)
            for bank, part in reversed(banks[t]):
                if t == 0:
                    nc.vector.tensor_scalar(out=s_rows[t][:, part], in0=bank, scalar1=0.0625, scalar2=None, op0=ALU.mult)
                else:
                    nc.scalar.activation(out=s_rows[t][:, part], in_=bank, func=ACT.Copy, scale=0.0625)
            st_win[t] = rows.tile([P, WIN], F32, tag="win_b", name="st_win")
            nc.vector.tensor_tensor(out=st_win[t][:, :S], in0=neg_win[t][:].indirect(l5[:]), in1=s_rows[t][:], op=ALU.add)

        def excess(t):
            st_twin[t] = rows.tile([P, S], F32, tag="term0", name="st_twin")
            nc.scalar.copy(out=st_twin[t][:], in_=st_win[t][:, :S])
            rise[t] = rows.tile([P, S], F32, tag="term1", name="rise")
            nc.vector.tensor_tensor(out=rise[t][:], in0=st_win[t][:].indirect(l6[:]), in1=st_twin[t][:], op=ALU.subtract)

        def clip(t):
            nc.scalar.activation(out=rise[t][:], in_=rise[t][:], func=ACT.Relu)
            banks[t] = psum.tile([P, S], F32, tag="bank", name="su_bank")
            turn(banks[t], [st_twin[t], rise[t]])

        def turn_back(t):
            su_turned[t] = rows.tile([P, S], F32, tag="weight0", name="su_turned")
            nc.scalar.copy(out=su_turned[t][:], in_=banks[t][:])
            turn(banks[t], [su_turned[t]])

        def halve(t, source):
            half_win[t] = rows.tile([P, S], F32, tag="win_c", name="half_win")
            nc.scalar.activation(out=half_win[t][:], in_=source, func=ACT.Copy, scale=0.5)

        def leave_bank(t):
            su[t] = rows.tile([P, S], F32, tag="twin_b", name="su")
            nc.scalar.copy(out=su[t][:], in_=banks[t][:])
            halve(t, banks[t][:])

        step(0)
        step(1)
        excess(0)
        step(2)
        excess(1)
        clip(0)
        step(3)
        turn_back(0)
        clip(1)
        leave_bank(0)
        turn_back(1)
        for t in (2, 3):
            nc.vector.tensor_copy(out=s_rows[t ^ 1][:], in_=st_win[t][:].indirect(l6[:]))
        for t in (2, 3):
            su[t] = rows.tile([P, S], F32, tag="twin_b", name="su")
            nc.vector.tensor_tensor(out=su[t][:], in0=st_win[t][:, :S], in1=s_rows[t ^ 1][:], op=ALU.max)
        halve(2, su[2][:])
        leave_bank(1)
        halve(3, su[3][:])

        out_rows = out_0.rearrange("(p t) n -> p t n", t=PACK)
        words = out_1[0].rearrange("p n t -> p (n t)").bitcast(I32)
        oq = keep.tile([P, S], I32, align_bytes=64)
        oqs = keep.tile([P, S], U8, align_bytes=64)
        for lo, hi in CHUNKS:
            res = keep.tile([P, PACK, hi - lo], F32, name="res%d" % lo)
            for t in (0, 2, 1, 3):
                nc.vector.tensor_tensor(
                    out=res[:, t, :], in0=half_win[t][:].indirect(l7[:, lo // 16 : hi // 16]), in1=su[t][:, lo:hi], op=ALU.add
                )
            nc.sync.dma_start(out_rows[:, :, lo:hi], res[:])
            res_bf = keep.tile([P, PACK * (hi - lo)], BF16, align_bytes=64, name="res_bf%d" % lo)
            dst = res_bf[:].rearrange("p (m i j) -> p m j i", i=PACK, j=PACK)
            src = res[:].rearrange("p j (m i) -> p m j i", i=PACK)
            if hi < S:
                nc.scalar.copy(out=dst, in_=src)
            else:
                nc.vector.tensor_copy(out=dst, in_=src)
            nc.vector.quantize_mx(out=oq[:, lo:hi].bitcast(FP8X4), scales=oqs[:, lo:hi], in_=res_bf[:])
            nc.sync.dma_start(words[:, lo:hi], oq[:, lo:hi])
        for q in range(4):
            queue = nc.scalar if q % 2 else nc.sync
            queue.dma_start(out_2[0, 4 * q : 4 * q + 4, :].bitcast(I32), oqs[32 * q : 32 * q + 4, :].bitcast(I32))
